import numpy as np
import ml_dtypes


def mxq(x, axis, fmt="e4m3"):
    dtype, down = {"e4m3": (ml_dtypes.float8_e4m3fn, 7), "e5m2": (ml_dtypes.float8_e5m2, 14)}[fmt]
    v = np.moveaxis(np.asarray(x, np.float32).astype(ml_dtypes.bfloat16).astype(np.float64), axis, -1)
    blocks = v.reshape(v.shape[:-1] + (-1, 32))
    amax = np.abs(blocks).max(-1, keepdims=True)
    byte = np.maximum(np.where(amax > 0, np.frexp(amax)[1] - 1 + 127, 0) - down, 1)
    scale = np.exp2(byte - 127.0)
    codes = (blocks / scale).astype(np.float32).astype(dtype).astype(np.float64)
    return np.moveaxis((codes * scale).reshape(v.shape), -1, axis)


WIDE = False


def mx_kscale(k):
    if not WIDE:
        return np.ones(k)
    levels = np.array([10, -10, 5, -5, 0])
    if k % 512:
        return np.exp2(np.random.permutation(np.resize(levels, k // 32))).repeat(32)
    a = np.empty((k // 512, 16))
    for p in range(k // 512):
        a[p, :8] = np.random.permutation(np.resize(levels, 8))
        for g in range(8):
            far = levels[np.abs(levels - a[p, g]) >= 10]
            a[p, g + 8] = far[np.random.randint(len(far))]
    return np.exp2(a.ravel()).repeat(32)


BF16 = ml_dtypes.bfloat16


def bf(x):
    return np.asarray(x, np.float32).astype(BF16)


def f64(x):
    return np.asarray(x).astype(np.float64)


E2M1 = np.array([0.0, 0.5, 1.0, 1.5, 2.0, 3.0, 4.0, 6.0, -0.0, -0.5, -1.0, -1.5, -2.0, -3.0, -4.0, -6.0])


def pack_weight(w, fmt):
    k, n = w.shape
    w = f64(bf(w)).reshape(k // 32, 32, n)
    amax = np.abs(w).max(1)
    if fmt == "e4m3":
        byte = np.frexp(amax)[1] - 1 + 127 - 7
    else:
        mant, ex = np.frexp(amax / 6.0)
        byte = np.where(mant > 0.5, ex, ex - 1) + 127
    byte = np.clip(np.where(amax > 0, byte, 1), 1, 254)
    scaled = (w * np.exp2(127.0 - byte)[:, None, :]).reshape(k, n).astype(np.float32)
    by_word = np.ascontiguousarray(scaled.reshape(k // 512, 128, 4, n).transpose(0, 1, 3, 2))
    if fmt == "e4m3":
        words = by_word.astype(ml_dtypes.float8_e4m3fn).view(np.uint8)
    else:
        c = by_word.astype(ml_dtypes.float4_e2m1fn).view(np.uint8) & 0xF
        words = c[..., 0::2] | (c[..., 1::2] << 4)
    return np.ascontiguousarray(words), np.ascontiguousarray(byte.astype(np.uint8).reshape(k // 512, 16, n))


def unpack_weight(words, scales, fmt):
    g, p, n, _ = words.shape
    if fmt == "e4m3":
        vals = np.ascontiguousarray(words).view(ml_dtypes.float8_e4m3fn).astype(np.float64)
    else:
        nib = np.empty((g, p, n, 4), np.uint8)
        nib[..., 0::2] = words & 0xF
        nib[..., 1::2] = words >> 4
        vals = E2M1[nib]
    vals = vals * np.repeat(np.exp2(scales.astype(np.float64) - 127.0), 8, axis=1)[..., None]
    return vals.transpose(0, 1, 3, 2).reshape(g * 512, n)
def pack4(w):
    words, scales = pack_weight(w, "e2m1")
    return words.reshape(words.shape[0], 128, -1), scales


def unpack4(words, scales):
    return unpack_weight(words.reshape(words.shape[0], 128, -1, 2), scales, "e2m1")


M, K, F, L, D = 1024, 512, 1024, 6, 256
P = L * D
MAX_FREQ = 1000.0


def setup_inputs():
    s, t, u = mx_kscale(K), mx_kscale(F), mx_kscale(M)
    level = np.random.random(M)
    phase = level[:, None] * MAX_FREQ ** np.linspace(0.0, 1.0, K // 2)
    emb = np.concatenate([np.cos(phase), np.sin(phase)], axis=1)
    w1 = np.random.standard_normal((K, F)) * 2.0 / np.sqrt(K)
    table = np.random.standard_normal((F, P)) / np.sqrt(F)
    table_words, table_scales = pack4(table / t[:, None])
    return {"emb": bf(emb * s),
            "w1": bf(w1 / s[:, None]),
            "gain": bf((1 + 0.1 * np.random.standard_normal(F)) * t),
            "table_words": table_words,
            "table_scales": table_scales,
            "level_weight": bf(np.exp(0.5 * np.random.standard_normal(M)) / np.sqrt(M) * u),
            "teacher": bf(np.random.standard_normal((M, P)) / u[:, None])}


def reference(emb, w1, gain, table_words, table_scales, level_weight, teacher):
    z = mxq(f64(emb), 1, "e4m3") @ mxq(f64(w1), 0, "e4m3")
    h = z / (1 + np.exp(-z))
    a = h * f64(gain)
    b = h * f64(level_weight)[:, None]
    bias = mxq(a, 1, "e4m3") @ unpack4(table_words, table_scales)
    moments = mxq(b, 0, "e4m3").T @ mxq(f64(teacher), 0, "e4m3")
    return bias, moments

@@ -1,0 +1,505 @@
+from contextlib import ExitStack
+
+import concourse.mybir as mybir
+from concourse.masks import make_identity
+
+M, K, F, C = 1024, 512, 1024, 1536
+FLOPS = 2 * M * K * F + 2 * M * F * C + 2 * F * M * C
+
+F32 = mybir.dt.float32
+BF16 = mybir.dt.bfloat16
+I32 = mybir.dt.int32
+U32 = mybir.dt.uint32
+U8 = mybir.dt.uint8
+FP8X4 = mybir.dt.float8_e4m3fn_x4
+FP4X4 = mybir.dt.float4_e2m1fn_x4
+SILU = mybir.ActivationFunctionType.Silu
+MULT = mybir.AluOpType.mult
+
+P = 128
+PACK = 4
+BANK = 512
+CHUNKS = C // BANK
+
+
+def tile_timestep_bias_table_calibration_s8_kernel(
+    tc, emb, w1, gain, table_words, table_scales, level_weight, teacher, out_0, out_1
+):
+    nc = tc.nc
+    emb_rows = emb.rearrange("(g p t) k -> g p t k", g=2, t=PACK)
+    w1_rows = w1.rearrange("(p t) f -> p t f", t=PACK)
+    teacher_rows = teacher.rearrange("(g p t) c -> g p t c", g=2, t=PACK)
+    bias_rows = out_0.rearrange("(g p t) c -> g t p c", g=2, t=PACK)
+    moment_rows = out_1.rearrange("(g p t) c -> g t p c", g=2, t=PACK)
+
+    with ExitStack() as ctx:
+        keep = ctx.enter_context(tc.tile_pool(name="keep", bufs=1))
+        stage = ctx.enter_context(tc.tile_pool(name="stage", bufs=3))
+        wide = ctx.enter_context(tc.tile_pool(name="wide", bufs=4))
+        results = ctx.enter_context(tc.tile_pool(name="results", bufs=7))
+        psum = ctx.enter_context(tc.psum_pool(name="psum", bufs=8))
+        ctx.enter_context(tc.manual_schedule())
+
+        ident = keep.tile([P, P], F32, name="ident")
+        warm = keep.tile([P, 2], F32, name="warm")
+        gain_sb = keep.tile([P, 2, PACK], BF16, name="gain_sb")
+        level_sb = keep.tile([P, 2, PACK], BF16, name="level_sb")
+        emb_raw = keep.tile([P, 8, K], BF16, name="emb_raw", align_bytes=64)
+        w1_raw = keep.tile([P, 2, PACK, BANK], BF16, name="w1_raw", align_bytes=64)
+        teacher_raw = keep.tile([P, 2, PACK, C], BF16, name="teacher_raw", align_bytes=64)
+        table_codes = keep.tile([P, 2, 2 * C], U8, name="table_codes", align_bytes=64)
+        table_plane = keep.tile([P, 2, C], U8, name="table_plane", align_bytes=64)
+        emb_codes = keep.tile([P, M], U32, name="emb_codes", align_bytes=64)
+        emb_plane = keep.tile([P, M], U8, name="emb_plane", align_bytes=64)
+        w1_codes = keep.tile([P, F], U32, name="w1_codes", align_bytes=64)
+        w1_plane = keep.tile([P, F], U8, name="w1_plane", align_bytes=64)
+        teacher_codes = keep.tile([P, 2, C], U32, name="teacher_codes", align_bytes=64)
+        teacher_plane = keep.tile([P, 2, C], U8, name="teacher_plane", align_bytes=64)
+        a_codes = keep.tile([P, 8, 2 * P], U32, name="a_codes", align_bytes=64)
+        a_plane = keep.tile([P, 8, 2 * P], U8, name="a_plane", align_bytes=64)
+        b_codes = keep.tile([P, 2, F], U32, name="b_codes", align_bytes=64)
+        b_plane = keep.tile([P, 2, F], U8, name="b_plane", align_bytes=64)
+        h = keep.tile([P, 8, F], F32, name="h", align_bytes=64)
+        held = {}
+
+        def bank_tile():
+            return psum.tile([P, BANK], F32, name="bank")
+
+        def interleave(engine, rows, packed):
+            src = rows.rearrange("p t (c i) -> p c t i", i=4)
+            dst = packed.rearrange("p (c i t) -> p c t i", i=4, t=PACK)
+            if engine is nc.scalar:
+                nc.scalar.copy(out=dst, in_=src)
+            else:
+                nc.vector.tensor_copy(out=dst, in_=src)
+
+        def quantize(codes, plane, packed):
+            nc.vector.quantize_mx(out=codes.bitcast(FP8X4), scales=plane, in_=packed)
+
+        def emb_turn(pair):
+            bank = bank_tile()
+            for s in range(2):
+                words = emb_raw[:, 2 * pair + s, :].bitcast(F32)
+                for u in range(2):
+                    at = (2 * s + u) * P
+                    nc.tensor.transpose(bank[:, at : at + P], words[:, u : 2 * P : 2], ident[:])
+            held["emb_turned", pair] = bank
+
+        def copy(engine, out, in_):
+            if engine is nc.scalar:
+                nc.scalar.copy(out=out, in_=in_)
+            else:
+                nc.vector.tensor_copy(out=out, in_=in_)
+
+        def emb_copy(engine, pair):
+            bank = held["emb_turned", pair]
+            packed = stage.tile([P, 2 * BANK], BF16, name="emb_packed", align_bytes=64)
+            copy(
+                engine,
+                packed[:].bitcast(F32).rearrange("p (s r u) -> p s r u", s=2, u=2),
+                bank[:].rearrange("p (s u r) -> p s r u", s=2, u=2),
+            )
+            held["emb", pair] = packed
+
+        def emb_quantize(pair):
+            cols = slice(2 * P * pair, 2 * P * (pair + 1))
+            quantize(emb_codes[:, cols], emb_plane[:, cols], held["emb", pair][:])
+
+        def w1_pack(engine, half, part):
+            if part == 0:
+                held["w1", half] = wide.tile([P, PACK * BANK], BF16, name="wide_packed", align_bytes=64)
+            interleave(
+                engine,
+                w1_raw[:, half, :, 2 * P * part : 2 * P * (part + 1)],
+                held["w1", half][:, 2 * BANK * part : 2 * BANK * (part + 1)],
+            )
+
+        def w1_quantize(half):
+            cols = slice(BANK * half, BANK * (half + 1))
+            quantize(w1_codes[:, cols], w1_plane[:, cols], held["w1", half][:])
+
+        def teacher_pack(engine, g, n, half):
+            if half == 0:
+                held["teacher", g, n] = wide.tile([P, PACK * BANK], BF16, name="wide_packed", align_bytes=64)
+            at = BANK * n + 2 * P * half
+            interleave(
+                engine,
+                teacher_raw[:, g, :, at : at + 2 * P],
+                held["teacher", g, n][:, 2 * BANK * half : 2 * BANK * (half + 1)],
+            )
+
+        def teacher_quantize(g, n):
+            cols = slice(BANK * n, BANK * (n + 1))
+            quantize(teacher_codes[:, g, cols], teacher_plane[:, g, cols], held["teacher", g, n][:])
+
+        def hidden(i, half):
+            rows = slice(P * i, P * (i + 1))
+            cols = slice(BANK * half, BANK * (half + 1))
+            bank = bank_tile()
+            nc.tensor.matmul_mx(
+                out=bank[:],
+                lhsT=emb_codes[:, rows].bitcast(FP8X4),
+                lhsT_scale=emb_plane[:, rows],
+                rhs=w1_codes[:, cols].bitcast(FP8X4),
+                rhs_scale=w1_plane[:, cols],
+                start=True,
+                stop=True,
+            )
+            held["z", i, half] = bank
+
+        def silu(i, half):
+            cols = slice(BANK * half, BANK * (half + 1))
+            bank = held["z", i, half]
+            nc.scalar.activation(
+                out=h[:, i, cols].rearrange("p (t m) -> p t m", t=PACK),
+                in_=bank[:].rearrange("p (m t) -> p t m", t=PACK),
+                func=SILU,
+            )
+
+        def h_turn(i, half):
+            bank = bank_tile()
+            for t in range(PACK):
+                at = BANK * half + P * t
+                nc.tensor.transpose(bank[:, P * t : P * (t + 1)], h[:, i, at : at + P], ident[:])
+            held["turned", i, half] = bank
+
+        def a_scale(i, half):
+            if half == 0:
+                held["a", i] = stage.tile([P, 2 * BANK], BF16, name="a_packed", align_bytes=64)
+            nc.vector.tensor_tensor(
+                out=held["a", i][:, BANK * half : BANK * (half + 1)].rearrange("p (n t) -> p n t", t=PACK),
+                in0=held["turned", i, half][:].rearrange("p (t n) -> p n t", t=PACK),
+                in1=gain_sb[:, half, :].unsqueeze(1).to_broadcast([P, P, PACK]),
+                op=MULT,
+            )
+
+        def a_quantize(i):
+            quantize(a_codes[:, i, :], a_plane[:, i, :], held["a", i][:])
+
+        def b_scale(g, q):
+            packed = stage.tile([P, 2 * BANK], BF16, name="b_packed", align_bytes=64)
+            rows = h[:, PACK * g : PACK * (g + 1), 2 * P * q : 2 * P * (q + 1)]
+            nc.vector.tensor_tensor(
+                out=packed[:].rearrange("p (c i t) -> p c t i", i=4, t=PACK),
+                in0=rows.rearrange("p t (c i) -> p c t i", i=4),
+                in1=level_sb[:, g, :].unsqueeze(1).unsqueeze(3).to_broadcast([P, 64, PACK, 4]),
+                op=MULT,
+            )
+            held["b", g, q] = packed
+
+        def b_quantize(g, q):
+            cols = slice(2 * P * q, 2 * P * (q + 1))
+            quantize(b_codes[:, g, cols], b_plane[:, g, cols], held["b", g, q][:])
+
+        def bias_mm(i, n):
+            bank = bank_tile()
+            for g in range(2):
+                nc.tensor.matmul_mx(
+                    out=bank[:],
+                    lhsT=a_codes[:, i, P * g : P * (g + 1)].bitcast(FP8X4),
+                    lhsT_scale=a_plane[:, i, P * g : P * (g + 1)],
+                    rhs=table_codes[:, g, 2 * BANK * n : 2 * BANK * (n + 1)].bitcast(FP4X4),
+                    rhs_scale=table_plane[:, g, BANK * n : BANK * (n + 1)],
+                    start=(g == 0),
+                    stop=(g == 1),
+                )
+            held["sum", 0, i, n] = bank
+
+        def moment_mm(j, n):
+            bank = bank_tile()
+            for g in range(2):
+                nc.tensor.matmul_mx(
+                    out=bank[:],
+                    lhsT=b_codes[:, g, P * j : P * (j + 1)].bitcast(FP8X4),
+                    lhsT_scale=b_plane[:, g, P * j : P * (j + 1)],
+                    rhs=teacher_codes[:, g, BANK * n : BANK * (n + 1)].bitcast(FP8X4),
+                    rhs_scale=teacher_plane[:, g, BANK * n : BANK * (n + 1)],
+                    start=(g == 0),
+                    stop=(g == 1),
+                )
+            held["sum", 1, j, n] = bank
+
+        def empty(engine, which, i, n):
+            if n == 0:
+                held["result", which, i] = results.tile([P, C], F32, name="result")
+            copy(engine, held["result", which, i][:, BANK * n : BANK * (n + 1)], held["sum", which, i, n][:])
+
+        def store(which, i, first, last):
+            rows = (bias_rows, moment_rows)[which][i // PACK, i % PACK]
+            cols = slice(BANK * first, BANK * last)
+            nc.sync.dma_start(out=rows[:, cols], in_=held["result", which, i][:, cols])
+
+        V, S = nc.vector, nc.scalar
+        nc.sync.dma_start(out=emb_raw[:, 0:2, :], in_=emb_rows[0, :, 0:2, :])
+        nc.sync.dma_start(out=w1_raw[:, 0], in_=w1_rows[:, :, :BANK])
+        nc.scalar.dma_start(out=gain_sb[:], in_=gain.rearrange("(g p t) -> p g t", g=2, t=PACK))
+        nc.scalar.dma_start(out=level_sb[:], in_=level_weight.rearrange("(g p t) -> p g t", g=2, t=PACK))
+        nc.vector.memset(table_plane[:].rearrange("p g c -> p (g c)").bitcast(I32), 0)
+        nc.vector.memset(warm[:], 0.0)
+        make_identity(nc, ident[:])
+        nc.scalar.activation(out=warm[:, 1:2], in_=warm[:, 0:1], func=SILU)
+        nc.sync.dma_start(out=emb_raw[:, 2:4, :], in_=emb_rows[0, :, 2:4, :])
+        nc.sync.dma_start(out=w1_raw[:, 1], in_=w1_rows[:, :, BANK:])
+        nc.sync.dma_start(
+            out=table_plane[64 : 68].bitcast(I32),
+            in_=table_scales[:, 8 : 12, :].rearrange("g r c -> r g c").bitcast(I32),
+        )
+        nc.sync.dma_start(
+            out=table_plane[0 : 4].bitcast(I32),
+            in_=table_scales[:, 0 : 4, :].rearrange("g r c -> r g c").bitcast(I32),
+        )
+        nc.sync.dma_start(
+            out=table_plane[96 : 100].bitcast(I32),
+            in_=table_scales[:, 12 : 16, :].rearrange("g r c -> r g c").bitcast(I32),
+        )
+        nc.sync.dma_start(out=teacher_raw[:, 0, :, :BANK], in_=teacher_rows[0, :, :, :BANK])
+        nc.sync.dma_start(
+            out=table_plane[32 : 36].bitcast(I32),
+            in_=table_scales[:, 4 : 8, :].rearrange("g r c -> r g c").bitcast(I32),
+        )
+        nc.sync.dma_start(out=emb_raw[:, 4:8, :], in_=emb_rows[1])
+        nc.sync.dma_start(out=table_codes[:], in_=table_words.rearrange("g p n -> p g n"))
+        nc.sync.dma_start(out=teacher_raw[:, 0, :, BANK:], in_=teacher_rows[0, :, :, BANK:])
+        nc.sync.dma_start(out=teacher_raw[:, 1], in_=teacher_rows[1])
+        emb_turn(0)
+        emb_copy(V, 0)
+        w1_pack(S, 0, 0)
+        emb_quantize(0)
+        emb_turn(1)
+        emb_copy(S, 1)
+        w1_pack(V, 0, 1)
+        w1_quantize(0)
+        emb_quantize(1)
+        w1_pack(V, 1, 0)
+        hidden(0, 0)
+        w1_pack(S, 1, 1)
+        w1_quantize(1)
+        hidden(1, 0)
+        hidden(2, 0)
+        hidden(3, 0)
+        teacher_pack(V, 0, 0, 0)
+        silu(0, 0)
+        teacher_pack(V, 0, 0, 1)
+        silu(1, 0)
+        hidden(0, 1)
+        silu(2, 0)
+        teacher_quantize(0, 0)
+        hidden(1, 1)
+        h_turn(0, 0)
+        silu(0, 1)
+        a_scale(0, 0)
+        h_turn(0, 1)
+        silu(3, 0)
+        hidden(2, 1)
+        hidden(3, 1)
+        silu(1, 1)
+        a_scale(0, 1)
+        silu(3, 1)
+        h_turn(1, 0)
+        silu(2, 1)
+        h_turn(1, 1)
+        emb_turn(2)
+        a_quantize(0)
+        emb_copy(S, 2)
+        a_scale(1, 0)
+        bias_mm(0, 0)
+        bias_mm(0, 1)
+        b_scale(0, 0)
+        bias_mm(0, 2)
+        empty(S, 0, 0, 0)
+        emb_turn(3)
+        teacher_pack(S, 0, 1, 0)
+        h_turn(2, 0)
+        a_scale(1, 1)
+        h_turn(2, 1)
+        emb_quantize(2)
+        empty(V, 0, 0, 1)
+        empty(S, 0, 0, 2)
+        hidden(4, 0)
+        emb_copy(S, 3)
+        a_quantize(1)
+        hidden(4, 1)
+        bias_mm(1, 0)
+        bias_mm(1, 1)
+        bias_mm(1, 2)
+        a_scale(2, 0)
+        silu(4, 0)
+        h_turn(3, 0)
+        a_scale(2, 1)
+        teacher_pack(V, 0, 2, 0)
+        teacher_pack(V, 0, 1, 1)
+        h_turn(3, 1)
+        emb_quantize(3)
+        silu(4, 1)
+        hidden(5, 0)
+        hidden(5, 1)
+        a_quantize(2)
+        teacher_pack(V, 1, 1, 0)
+        empty(S, 0, 1, 0)
+        empty(S, 0, 1, 1)
+        bias_mm(2, 0)
+        empty(S, 0, 1, 2)
+        bias_mm(2, 1)
+        bias_mm(2, 2)
+        a_scale(3, 0)
+        h_turn(4, 0)
+        store(0, 0, 0, 3)
+        h_turn(4, 1)
+        teacher_pack(S, 1, 1, 1)
+        a_scale(3, 1)
+        b_quantize(0, 0)
+        silu(5, 1)
+        silu(5, 0)
+        empty(S, 0, 2, 0)
+        hidden(6, 0)
+        hidden(6, 1)
+        teacher_quantize(1, 1)
+        teacher_quantize(0, 1)
+        a_quantize(3)
+        empty(S, 0, 2, 1)
+        a_scale(4, 0)
+        a_scale(4, 1)
+        teacher_pack(V, 1, 0, 0)
+        bias_mm(3, 0)
+        empty(S, 0, 2, 2)
+        bias_mm(3, 1)
+        bias_mm(3, 2)
+        silu(6, 0)
+        teacher_pack(V, 0, 2, 1)
+        h_turn(5, 0)
+        empty(S, 0, 3, 0)
+        a_quantize(4)
+        h_turn(5, 1)
+        a_scale(5, 0)
+        empty(S, 0, 3, 1)
+        a_scale(5, 1)
+        hidden(7, 0)
+        store(0, 1, 0, 3)
+        hidden(7, 1)
+        teacher_pack(V, 1, 0, 1)
+        silu(6, 1)
+        empty(S, 0, 3, 2)
+        a_quantize(5)
+        bias_mm(4, 0)
+        silu(7, 0)
+        bias_mm(4, 1)
+        empty(S, 0, 4, 0)
+        bias_mm(4, 2)
+        empty(S, 0, 4, 1)
+        h_turn(6, 0)
+        empty(S, 0, 4, 2)
+        store(0, 2, 0, 3)
+        silu(7, 1)
+        teacher_pack(S, 1, 2, 0)
+        h_turn(6, 1)
+        store(0, 3, 0, 3)
+        bias_mm(5, 0)
+        empty(S, 0, 5, 0)
+        b_scale(1, 0)
+        teacher_pack(V, 1, 2, 1)
+        bias_mm(5, 1)
+        a_scale(6, 0)
+        a_scale(6, 1)
+        a_quantize(6)
+        teacher_quantize(1, 0)
+        b_quantize(1, 0)
+        empty(S, 0, 5, 1)
+        bias_mm(5, 2)
+        bias_mm(6, 0)
+        teacher_quantize(0, 2)
+        bias_mm(6, 1)
+        teacher_quantize(1, 2)
+        empty(S, 0, 5, 2)
+        empty(S, 0, 6, 0)
+        store(0, 4, 0, 3)
+        store(0, 5, 0, 3)
+        empty(S, 0, 6, 1)
+        b_scale(1, 1)
+        bias_mm(6, 2)
+        b_scale(0, 1)
+        b_quantize(1, 1)
+        b_quantize(0, 1)
+        b_scale(1, 2)
+        moment_mm(0, 0)
+        empty(S, 0, 6, 2)
+        empty(S, 1, 0, 0)
+        moment_mm(0, 1)
+        empty(S, 1, 0, 1)
+        b_scale(0, 2)
+        moment_mm(0, 2)
+        moment_mm(1, 0)
+        moment_mm(1, 1)
+        moment_mm(1, 2)
+        empty(S, 1, 0, 2)
+        moment_mm(2, 0)
+        moment_mm(2, 1)
+        empty(S, 1, 1, 0)
+        moment_mm(2, 2)
+        moment_mm(3, 0)
+        empty(S, 1, 1, 1)
+        b_quantize(1, 2)
+        moment_mm(3, 1)
+        b_quantize(0, 2)
+        store(0, 6, 0, 3)
+        empty(V, 1, 3, 0)
+        moment_mm(3, 2)
+        empty(S, 1, 1, 2)
+        b_scale(0, 3)
+        moment_mm(4, 0)
+        moment_mm(4, 1)
+        empty(S, 1, 2, 0)
+        b_scale(1, 3)
+        empty(S, 1, 2, 1)
+        moment_mm(4, 2)
+        b_quantize(0, 3)
+        empty(S, 1, 2, 2)
+        empty(S, 1, 3, 1)
+        empty(S, 1, 3, 2)
+        empty(S, 1, 4, 0)
+        moment_mm(5, 0)
+        empty(S, 1, 4, 1)
+        empty(S, 1, 4, 2)
+        moment_mm(5, 1)
+        moment_mm(5, 2)
+        h_turn(7, 0)
+        empty(V, 1, 5, 0)
+        h_turn(7, 1)
+        b_quantize(1, 3)
+        store(1, 0, 0, 3)
+        moment_mm(6, 0)
+        a_scale(7, 0)
+        empty(S, 1, 5, 1)
+        moment_mm(6, 1)
+        a_scale(7, 1)
+        moment_mm(6, 2)
+        store(1, 1, 0, 3)
+        moment_mm(7, 0)
+        a_quantize(7)
+        empty(S, 1, 5, 2)
+        moment_mm(7, 1)
+        moment_mm(7, 2)
+        empty(S, 1, 6, 0)
+        store(1, 2, 0, 3)
+        bias_mm(7, 0)
+        store(1, 3, 0, 3)
+        bias_mm(7, 1)
+        empty(V, 1, 6, 1)
+        store(1, 4, 0, 3)
+        store(1, 5, 0, 3)
+        store(1, 6, 0, 1)
+        empty(S, 1, 6, 2)
+        bias_mm(7, 2)
+        store(1, 6, 1, 2)
+        empty(S, 0, 7, 0)
+        store(1, 6, 2, 3)
+        empty(V, 1, 7, 0)
+        store(1, 7, 0, 1)
+        empty(V, 1, 7, 1)
+        store(1, 7, 1, 2)
+        empty(V, 1, 7, 2)
+        store(1, 7, 2, 3)
+        store(0, 7, 0, 1)
+        empty(V, 0, 7, 1)
+        empty(S, 0, 7, 2)
+        store(0, 7, 1, 2)
+        store(0, 7, 2, 3)

@@ -42,11 +42,15 @@ def tile_timestep_bias_table_calibration_s8_kernel(
 
         ident = keep.tile([P, P], F32, name="ident")
         warm = keep.tile([P, 2], F32, name="warm")
-        gain_sb = keep.tile([P, 2, PACK], BF16, name="gain_sb")
-        level_sb = keep.tile([P, 2, PACK], BF16, name="level_sb")
+        factor_rows = keep.tile([P, BANK], BF16, name="factor_rows")
+        factors = keep.tile([P, 4 * PACK], BF16, name="factors")
+        gain_sb = factors[:, : 2 * PACK].rearrange("p (g t) -> p g t", t=PACK)
+        level_sb = factors[:, 2 * PACK :].rearrange("p (g t) -> p g t", t=PACK)
         emb_raw = keep.tile([P, 8, K], BF16, name="emb_raw", align_bytes=64)
         w1_raw = keep.tile([P, 2, PACK, BANK], BF16, name="w1_raw", align_bytes=64)
-        teacher_raw = keep.tile([P, 2, PACK, C], BF16, name="teacher_raw", align_bytes=64)
+        teacher_first = keep.tile([P, PACK, BANK], BF16, name="teacher_first", align_bytes=64)
+        teacher_rest = keep.tile([P, PACK, C - BANK], BF16, name="teacher_rest", align_bytes=64)
+        teacher_late = keep.tile([P, PACK, C], BF16, name="teacher_late", align_bytes=64)
         table_codes = keep.tile([P, 2, 2 * C], U8, name="table_codes", align_bytes=64)
         table_plane = keep.tile([P, 2, C], U8, name="table_plane", align_bytes=64)
         emb_codes = keep.tile([P, M], U32, name="emb_codes", align_bytes=64)
@@ -57,9 +61,9 @@ def tile_timestep_bias_table_calibration_s8_kernel(
         teacher_plane = keep.tile([P, 2, C], U8, name="teacher_plane", align_bytes=64)
         a_codes = keep.tile([P, 8, 2 * P], U32, name="a_codes", align_bytes=64)
         a_plane = keep.tile([P, 8, 2 * P], U8, name="a_plane", align_bytes=64)
-        b_codes = keep.tile([P, 2, F], U32, name="b_codes", align_bytes=64)
-        b_plane = keep.tile([P, 2, F], U8, name="b_plane", align_bytes=64)
-        h = keep.tile([P, 8, F], F32, name="h", align_bytes=64)
+        b_codes = keep.tile([P, 4, BANK], U32, name="b_codes", align_bytes=64)
+        b_plane = keep.tile([P, 4, BANK], U8, name="b_plane", align_bytes=64)
+        h = keep.tile([P, 2, 8, BANK], F32, name="h", align_bytes=64)
         held = {}
 
         def bank_tile():
@@ -75,6 +79,16 @@ def tile_timestep_bias_table_calibration_s8_kernel(
 
         def quantize(codes, plane, packed):
             nc.vector.quantize_mx(out=codes.bitcast(FP8X4), scales=plane, in_=packed)
+
+        def factors_turn():
+            bank = bank_tile()
+            words = factor_rows[:].bitcast(F32)
+            for u in range(2):
+                nc.tensor.transpose(bank[:, u * P : (u + 1) * P], words[:, u : 2 * P : 2], ident[:])
+            nc.scalar.copy(
+                out=factors[:].bitcast(F32).rearrange("p (r u) -> p r u", u=2),
+                in_=bank[:, : 2 * P].rearrange("p (u r) -> p r u", u=2)[:, :4, :],
+            )
 
         def emb_turn(pair):
             bank = bank_tile()
@@ -108,10 +122,10 @@ def tile_timestep_bias_table_calibration_s8_kernel(
         def w1_pack(engine, half, part):
             if part == 0:
                 held["w1", half] = wide.tile([P, PACK * BANK], BF16, name="wide_packed", align_bytes=64)
-            interleave(
+            copy(
                 engine,
-                w1_raw[:, half, :, 2 * P * part : 2 * P * (part + 1)],
-                held["w1", half][:, 2 * BANK * part : 2 * BANK * (part + 1)],
+                held["w1", half][:, 2 * BANK * part : 2 * BANK * (part + 1)].rearrange("p (t m j) -> p t m j", t=2, j=PACK),
+                w1_raw[:, half].rearrange("p j (m t) -> p t m j", t=PACK)[:, 2 * part : 2 * part + 2],
             )
 
         def w1_quantize(half):
@@ -122,9 +136,15 @@ def tile_timestep_bias_table_calibration_s8_kernel(
             if half == 0:
                 held["teacher", g, n] = wide.tile([P, PACK * BANK], BF16, name="wide_packed", align_bytes=64)
             at = BANK * n + 2 * P * half
+            if g == 1:
+                rows = teacher_late[:, :, at : at + 2 * P]
+            elif n == 0:
+                rows = teacher_first[:, :, at : at + 2 * P]
+            else:
+                rows = teacher_rest[:, :, at - BANK : at - BANK + 2 * P]
             interleave(
                 engine,
-                teacher_raw[:, g, :, at : at + 2 * P],
+                rows,
                 held["teacher", g, n][:, 2 * BANK * half : 2 * BANK * (half + 1)],
             )
 
@@ -148,19 +168,17 @@ def tile_timestep_bias_table_calibration_s8_kernel(
             held["z", i, half] = bank
 
         def silu(i, half):
-            cols = slice(BANK * half, BANK * (half + 1))
             bank = held["z", i, half]
             nc.scalar.activation(
-                out=h[:, i, cols].rearrange("p (t m) -> p t m", t=PACK),
-                in_=bank[:].rearrange("p (m t) -> p t m", t=PACK),
+                out=h[:, half, i, :],
+                in_=bank[:],
                 func=SILU,
             )
 
         def h_turn(i, half):
             bank = bank_tile()
             for t in range(PACK):
-                at = BANK * half + P * t
-                nc.tensor.transpose(bank[:, P * t : P * (t + 1)], h[:, i, at : at + P], ident[:])
+                nc.tensor.transpose(bank[:, P * t : P * (t + 1)], h[:, half, i, P * t : P * (t + 1)], ident[:])
             held["turned", i, half] = bank
 
         def a_scale(i, half):
@@ -177,19 +195,18 @@ def tile_timestep_bias_table_calibration_s8_kernel(
             quantize(a_codes[:, i, :], a_plane[:, i, :], held["a", i][:])
 
         def b_scale(g, q):
-            packed = stage.tile([P, 2 * BANK], BF16, name="b_packed", align_bytes=64)
-            rows = h[:, PACK * g : PACK * (g + 1), 2 * P * q : 2 * P * (q + 1)]
+            if g == 0:
+                held["b", q] = wide.tile([P, PACK * BANK], BF16, name="b_packed", align_bytes=64)
+            rows = h[:, q // 2, PACK * g : PACK * (g + 1), 2 * P * (q % 2) : 2 * P * (q % 2 + 1)]
             nc.vector.tensor_tensor(
-                out=packed[:].rearrange("p (c i t) -> p c t i", i=4, t=PACK),
-                in0=rows.rearrange("p t (c i) -> p c t i", i=4),
-                in1=level_sb[:, g, :].unsqueeze(1).unsqueeze(3).to_broadcast([P, 64, PACK, 4]),
+                out=held["b", q][:, 2 * BANK * g : 2 * BANK * (g + 1)].rearrange("p (c i t) -> p c t i", i=2, t=PACK),
+                in0=rows.rearrange("p t (c i) -> p c t i", i=2),
+                in1=level_sb[:, g, :].unsqueeze(1).unsqueeze(3).to_broadcast([P, P, PACK, 2]),
                 op=MULT,
             )
-            held["b", g, q] = packed
 
-        def b_quantize(g, q):
-            cols = slice(2 * P * q, 2 * P * (q + 1))
-            quantize(b_codes[:, g, cols], b_plane[:, g, cols], held["b", g, q][:])
+        def b_quantize(q):
+            quantize(b_codes[:, q, :], b_plane[:, q, :], held["b", q][:])
 
         def bias_mm(i, n):
             bank = bank_tile()
@@ -208,10 +225,11 @@ def tile_timestep_bias_table_calibration_s8_kernel(
         def moment_mm(j, n):
             bank = bank_tile()
             for g in range(2):
+                at = 2 * P * g + P * (j % 2)
                 nc.tensor.matmul_mx(
                     out=bank[:],
-                    lhsT=b_codes[:, g, P * j : P * (j + 1)].bitcast(FP8X4),
-                    lhsT_scale=b_plane[:, g, P * j : P * (j + 1)],
+                    lhsT=b_codes[:, j // 2, at : at + P].bitcast(FP8X4),
+                    lhsT_scale=b_plane[:, j // 2, at : at + P],
                     rhs=teacher_codes[:, g, BANK * n : BANK * (n + 1)].bitcast(FP8X4),
                     rhs_scale=teacher_plane[:, g, BANK * n : BANK * (n + 1)],
                     start=(g == 0),
@@ -232,274 +250,261 @@ def tile_timestep_bias_table_calibration_s8_kernel(
         V, S = nc.vector, nc.scalar
         nc.sync.dma_start(out=emb_raw[:, 0:2, :], in_=emb_rows[0, :, 0:2, :])
         nc.sync.dma_start(out=w1_raw[:, 0], in_=w1_rows[:, :, :BANK])
-        nc.scalar.dma_start(out=gain_sb[:], in_=gain.rearrange("(g p t) -> p g t", g=2, t=PACK))
-        nc.scalar.dma_start(out=level_sb[:], in_=level_weight.rearrange("(g p t) -> p g t", g=2, t=PACK))
+        nc.vector.memset(factor_rows[:].bitcast(I32), 0)
+        nc.scalar.dma_start(out=factor_rows[0:2, :], in_=gain.rearrange("(g k) -> g k", g=2))
+        nc.scalar.dma_start(out=factor_rows[2:4, :], in_=level_weight.rearrange("(g k) -> g k", g=2))
         nc.vector.memset(table_plane[:].rearrange("p g c -> p (g c)").bitcast(I32), 0)
         nc.vector.memset(warm[:], 0.0)
         make_identity(nc, ident[:])
         nc.scalar.activation(out=warm[:, 1:2], in_=warm[:, 0:1], func=SILU)
         nc.sync.dma_start(out=emb_raw[:, 2:4, :], in_=emb_rows[0, :, 2:4, :])
         nc.sync.dma_start(out=w1_raw[:, 1], in_=w1_rows[:, :, BANK:])
-        nc.sync.dma_start(
-            out=table_plane[64 : 68].bitcast(I32),
-            in_=table_scales[:, 8 : 12, :].rearrange("g r c -> r g c").bitcast(I32),
-        )
-        nc.sync.dma_start(
-            out=table_plane[0 : 4].bitcast(I32),
-            in_=table_scales[:, 0 : 4, :].rearrange("g r c -> r g c").bitcast(I32),
-        )
-        nc.sync.dma_start(
-            out=table_plane[96 : 100].bitcast(I32),
-            in_=table_scales[:, 12 : 16, :].rearrange("g r c -> r g c").bitcast(I32),
-        )
-        nc.sync.dma_start(out=teacher_raw[:, 0, :, :BANK], in_=teacher_rows[0, :, :, :BANK])
-        nc.sync.dma_start(
-            out=table_plane[32 : 36].bitcast(I32),
-            in_=table_scales[:, 4 : 8, :].rearrange("g r c -> r g c").bitcast(I32),
-        )
+        nc.sync.dma_start(out=teacher_first[:], in_=teacher_rows[0, :, :, :BANK])
         nc.sync.dma_start(out=emb_raw[:, 4:8, :], in_=emb_rows[1])
+        for r in range(4):
+            nc.sync.dma_start(
+                out=table_plane[r:P:32].bitcast(I32),
+                in_=table_scales[:, r:16:4, :].rearrange("g q c -> q g c").bitcast(I32),
+            )
         nc.sync.dma_start(out=table_codes[:], in_=table_words.rearrange("g p n -> p g n"))
-        nc.sync.dma_start(out=teacher_raw[:, 0, :, BANK:], in_=teacher_rows[0, :, :, BANK:])
-        nc.sync.dma_start(out=teacher_raw[:, 1], in_=teacher_rows[1])
+        nc.sync.dma_start(out=teacher_rest[:], in_=teacher_rows[0, :, :, BANK:])
+        nc.sync.dma_start(out=teacher_late[:], in_=teacher_rows[1])
         emb_turn(0)
         emb_copy(V, 0)
-        w1_pack(S, 0, 0)
-        emb_quantize(0)
+        w1_pack(V, 0, 0)
+        w1_pack(S, 0, 1)
         emb_turn(1)
-        emb_copy(S, 1)
-        w1_pack(V, 0, 1)
+        emb_quantize(0)
         w1_quantize(0)
+        emb_copy(S, 1)
+        hidden(0, 0)
         emb_quantize(1)
         w1_pack(V, 1, 0)
-        hidden(0, 0)
         w1_pack(S, 1, 1)
-        w1_quantize(1)
+        silu(0, 0)
         hidden(1, 0)
+        silu(1, 0)
+        teacher_pack(V, 0, 0, 0)
+        w1_quantize(1)
         hidden(2, 0)
         hidden(3, 0)
-        teacher_pack(V, 0, 0, 0)
-        silu(0, 0)
-        teacher_pack(V, 0, 0, 1)
-        silu(1, 0)
         hidden(0, 1)
+        teacher_pack(V, 0, 0, 1)
         silu(2, 0)
+        silu(0, 1)
         teacher_quantize(0, 0)
         hidden(1, 1)
+        factors_turn()
         h_turn(0, 0)
-        silu(0, 1)
-        a_scale(0, 0)
-        h_turn(0, 1)
-        silu(3, 0)
-        hidden(2, 1)
-        hidden(3, 1)
         silu(1, 1)
-        a_scale(0, 1)
-        silu(3, 1)
+        h_turn(0, 1)
+        hidden(2, 1)
+        a_scale(0, 0)
+        hidden(3, 1)
+        silu(3, 0)
         h_turn(1, 0)
-        silu(2, 1)
+        a_scale(0, 1)
+        a_quantize(0)
+        a_scale(1, 0)
         h_turn(1, 1)
         emb_turn(2)
-        a_quantize(0)
-        emb_copy(S, 2)
-        a_scale(1, 0)
         bias_mm(0, 0)
+        silu(3, 1)
+        silu(2, 1)
+        emb_copy(S, 2)
         bias_mm(0, 1)
         b_scale(0, 0)
         bias_mm(0, 2)
         empty(S, 0, 0, 0)
+        empty(S, 0, 0, 1)
+        empty(S, 0, 0, 2)
         emb_turn(3)
-        teacher_pack(S, 0, 1, 0)
         h_turn(2, 0)
         a_scale(1, 1)
-        h_turn(2, 1)
         emb_quantize(2)
-        empty(V, 0, 0, 1)
-        empty(S, 0, 0, 2)
-        hidden(4, 0)
-        emb_copy(S, 3)
         a_quantize(1)
+        teacher_pack(S, 0, 1, 0)
+        h_turn(2, 1)
+        emb_copy(S, 3)
+        hidden(4, 0)
         hidden(4, 1)
+        teacher_pack(V, 0, 2, 0)
+        silu(4, 0)
         bias_mm(1, 0)
         bias_mm(1, 1)
-        bias_mm(1, 2)
         a_scale(2, 0)
-        silu(4, 0)
-        h_turn(3, 0)
-        a_scale(2, 1)
-        teacher_pack(V, 0, 2, 0)
-        teacher_pack(V, 0, 1, 1)
-        h_turn(3, 1)
-        emb_quantize(3)
+        b_scale(0, 1)
+        bias_mm(1, 2)
         silu(4, 1)
+        h_turn(3, 0)
+        h_turn(3, 1)
+        a_scale(2, 1)
+        empty(S, 0, 1, 0)
+        emb_quantize(3)
+        a_quantize(2)
+        store(0, 0, 0, 3)
+        empty(S, 0, 1, 1)
         hidden(5, 0)
         hidden(5, 1)
-        a_quantize(2)
-        teacher_pack(V, 1, 1, 0)
-        empty(S, 0, 1, 0)
-        empty(S, 0, 1, 1)
         bias_mm(2, 0)
-        empty(S, 0, 1, 2)
         bias_mm(2, 1)
+        empty(S, 0, 1, 2)
         bias_mm(2, 2)
-        a_scale(3, 0)
         h_turn(4, 0)
-        store(0, 0, 0, 3)
-        h_turn(4, 1)
-        teacher_pack(S, 1, 1, 1)
-        a_scale(3, 1)
-        b_quantize(0, 0)
-        silu(5, 1)
         silu(5, 0)
-        empty(S, 0, 2, 0)
-        hidden(6, 0)
-        hidden(6, 1)
-        teacher_quantize(1, 1)
-        teacher_quantize(0, 1)
-        a_quantize(3)
-        empty(S, 0, 2, 1)
-        a_scale(4, 0)
-        a_scale(4, 1)
         teacher_pack(V, 1, 0, 0)
-        bias_mm(3, 0)
+        empty(S, 0, 2, 0)
+        a_scale(3, 0)
+        a_scale(3, 1)
+        empty(V, 0, 2, 1)
+        h_turn(4, 1)
+        a_quantize(3)
+        silu(5, 1)
         empty(S, 0, 2, 2)
+        teacher_pack(V, 0, 1, 1)
+        hidden(6, 0)
+        store(0, 1, 0, 3)
+        hidden(6, 1)
+        bias_mm(3, 0)
+        a_scale(4, 0)
         bias_mm(3, 1)
+        a_scale(4, 1)
         bias_mm(3, 2)
         silu(6, 0)
-        teacher_pack(V, 0, 2, 1)
         h_turn(5, 0)
         empty(S, 0, 3, 0)
-        a_quantize(4)
         h_turn(5, 1)
-        a_scale(5, 0)
         empty(S, 0, 3, 1)
-        a_scale(5, 1)
-        hidden(7, 0)
-        store(0, 1, 0, 3)
-        hidden(7, 1)
-        teacher_pack(V, 1, 0, 1)
         silu(6, 1)
+        teacher_pack(V, 1, 1, 0)
+        hidden(7, 0)
+        a_quantize(4)
+        a_scale(5, 0)
         empty(S, 0, 3, 2)
-        a_quantize(5)
+        hidden(7, 1)
+        a_scale(5, 1)
+        teacher_pack(V, 0, 2, 1)
+        teacher_quantize(0, 1)
         bias_mm(4, 0)
-        silu(7, 0)
         bias_mm(4, 1)
-        empty(S, 0, 4, 0)
-        bias_mm(4, 2)
-        empty(S, 0, 4, 1)
-        h_turn(6, 0)
-        empty(S, 0, 4, 2)
+        teacher_pack(V, 1, 0, 1)
+        silu(7, 0)
         store(0, 2, 0, 3)
-        silu(7, 1)
-        teacher_pack(S, 1, 2, 0)
+        bias_mm(4, 2)
+        a_quantize(5)
+        empty(S, 0, 4, 0)
+        h_turn(6, 0)
         h_turn(6, 1)
-        store(0, 3, 0, 3)
+        empty(S, 0, 4, 1)
+        empty(S, 0, 4, 2)
         bias_mm(5, 0)
-        empty(S, 0, 5, 0)
-        b_scale(1, 0)
-        teacher_pack(V, 1, 2, 1)
-        bias_mm(5, 1)
         a_scale(6, 0)
         a_scale(6, 1)
-        a_quantize(6)
-        teacher_quantize(1, 0)
-        b_quantize(1, 0)
-        empty(S, 0, 5, 1)
-        bias_mm(5, 2)
-        bias_mm(6, 0)
         teacher_quantize(0, 2)
+        b_scale(1, 0)
+        teacher_pack(S, 1, 2, 0)
+        a_quantize(6)
+        bias_mm(5, 1)
+        store(0, 3, 0, 3)
+        silu(7, 1)
+        b_quantize(0)
+        teacher_quantize(1, 0)
+        teacher_pack(S, 1, 1, 1)
+        teacher_pack(V, 1, 2, 1)
+        bias_mm(5, 2)
+        teacher_quantize(1, 1)
+        bias_mm(6, 0)
         bias_mm(6, 1)
+        empty(S, 0, 5, 0)
+        empty(S, 0, 5, 1)
+        bias_mm(6, 2)
         teacher_quantize(1, 2)
+        moment_mm(0, 0)
+        moment_mm(0, 1)
+        store(0, 4, 0, 3)
+        b_scale(1, 1)
         empty(S, 0, 5, 2)
         empty(S, 0, 6, 0)
-        store(0, 4, 0, 3)
-        store(0, 5, 0, 3)
-        empty(S, 0, 6, 1)
-        b_scale(1, 1)
-        bias_mm(6, 2)
-        b_scale(0, 1)
-        b_quantize(1, 1)
-        b_quantize(0, 1)
-        b_scale(1, 2)
-        moment_mm(0, 0)
-        empty(S, 0, 6, 2)
-        empty(S, 1, 0, 0)
-        moment_mm(0, 1)
-        empty(S, 1, 0, 1)
-        b_scale(0, 2)
         moment_mm(0, 2)
+        empty(S, 0, 6, 1)
+        empty(S, 0, 6, 2)
+        b_quantize(1)
         moment_mm(1, 0)
+        empty(S, 1, 0, 0)
         moment_mm(1, 1)
+        b_scale(0, 2)
         moment_mm(1, 2)
-        empty(S, 1, 0, 2)
         moment_mm(2, 0)
-        moment_mm(2, 1)
-        empty(S, 1, 1, 0)
-        moment_mm(2, 2)
-        moment_mm(3, 0)
-        empty(S, 1, 1, 1)
-        b_quantize(1, 2)
-        moment_mm(3, 1)
-        b_quantize(0, 2)
+        empty(S, 1, 0, 1)
+        store(0, 5, 0, 3)
+        b_scale(1, 2)
         store(0, 6, 0, 3)
-        empty(V, 1, 3, 0)
-        moment_mm(3, 2)
+        empty(S, 1, 0, 2)
+        empty(S, 1, 1, 0)
+        moment_mm(2, 1)
+        moment_mm(2, 2)
+        empty(S, 1, 1, 1)
+        empty(V, 1, 2, 0)
+        store(1, 0, 0, 3)
         empty(S, 1, 1, 2)
-        b_scale(0, 3)
-        moment_mm(4, 0)
-        moment_mm(4, 1)
-        empty(S, 1, 2, 0)
-        b_scale(1, 3)
+        b_quantize(2)
         empty(S, 1, 2, 1)
+        b_scale(0, 3)
+        moment_mm(3, 0)
+        moment_mm(3, 1)
+        moment_mm(3, 2)
+        moment_mm(4, 0)
+        empty(V, 1, 4, 0)
+        moment_mm(4, 1)
         moment_mm(4, 2)
-        b_quantize(0, 3)
         empty(S, 1, 2, 2)
-        empty(S, 1, 3, 1)
-        empty(S, 1, 3, 2)
-        empty(S, 1, 4, 0)
+        b_scale(1, 3)
+        store(1, 1, 0, 3)
         moment_mm(5, 0)
-        empty(S, 1, 4, 1)
-        empty(S, 1, 4, 2)
+        empty(V, 1, 5, 0)
+        empty(S, 1, 3, 0)
+        empty(S, 1, 3, 1)
         moment_mm(5, 1)
         moment_mm(5, 2)
+        b_quantize(3)
         h_turn(7, 0)
-        empty(V, 1, 5, 0)
+        empty(S, 1, 3, 2)
         h_turn(7, 1)
-        b_quantize(1, 3)
-        store(1, 0, 0, 3)
         moment_mm(6, 0)
         a_scale(7, 0)
-        empty(S, 1, 5, 1)
-        moment_mm(6, 1)
-        a_scale(7, 1)
-        moment_mm(6, 2)
-        store(1, 1, 0, 3)
-        moment_mm(7, 0)
-        a_quantize(7)
-        empty(S, 1, 5, 2)
-        moment_mm(7, 1)
-        moment_mm(7, 2)
-        empty(S, 1, 6, 0)
         store(1, 2, 0, 3)
-        bias_mm(7, 0)
+        empty(S, 1, 4, 1)
+        empty(S, 1, 4, 2)
+        moment_mm(6, 1)
+        empty(S, 1, 5, 1)
+        moment_mm(6, 2)
+        a_scale(7, 1)
+        empty(S, 1, 5, 2)
         store(1, 3, 0, 3)
-        bias_mm(7, 1)
-        empty(V, 1, 6, 1)
+        empty(S, 1, 6, 0)
         store(1, 4, 0, 3)
         store(1, 5, 0, 3)
-        store(1, 6, 0, 1)
-        empty(S, 1, 6, 2)
-        bias_mm(7, 2)
-        store(1, 6, 1, 2)
-        empty(S, 0, 7, 0)
-        store(1, 6, 2, 3)
-        empty(V, 1, 7, 0)
-        store(1, 7, 0, 1)
+        moment_mm(7, 0)
+        empty(V, 1, 6, 1)
+        moment_mm(7, 1)
+        empty(V, 1, 6, 2)
+        empty(S, 1, 7, 0)
+        a_quantize(7)
         empty(V, 1, 7, 1)
+        store(1, 6, 0, 1)
+        store(1, 6, 1, 2)
+        store(1, 6, 2, 3)
+        moment_mm(7, 2)
+        store(1, 7, 0, 1)
+        bias_mm(7, 0)
+        bias_mm(7, 1)
         store(1, 7, 1, 2)
         empty(V, 1, 7, 2)
         store(1, 7, 2, 3)
+        empty(S, 0, 7, 0)
+        empty(S, 0, 7, 1)
+        bias_mm(7, 2)
         store(0, 7, 0, 1)
-        empty(V, 0, 7, 1)
-        empty(S, 0, 7, 2)
         store(0, 7, 1, 2)
+        empty(S, 0, 7, 2)
         store(0, 7, 2, 3)

@@ -15,6 +15,7 @@ FP8X4 = mybir.dt.float8_e4m3fn_x4
 FP4X4 = mybir.dt.float4_e2m1fn_x4
 SILU = mybir.ActivationFunctionType.Silu
 MULT = mybir.AluOpType.mult
+ADD = mybir.AluOpType.add
 
 P = 128
 PACK = 4
@@ -64,6 +65,7 @@ def tile_timestep_bias_table_calibration_s8_kernel(
         b_codes = keep.tile([P, 4, BANK], U32, name="b_codes", align_bytes=64)
         b_plane = keep.tile([P, 4, BANK], U8, name="b_plane", align_bytes=64)
         h = keep.tile([P, 2, 8, BANK], F32, name="h", align_bytes=64)
+        ones = keep.tile([P, 64], F32, name="ones")
         held = {}
 
         def bank_tile():
@@ -132,20 +134,32 @@ def tile_timestep_bias_table_calibration_s8_kernel(
             cols = slice(BANK * half, BANK * (half + 1))
             quantize(w1_codes[:, cols], w1_plane[:, cols], held["w1", half][:])
 
-        def teacher_pack(engine, g, n, half):
-            if half == 0:
-                held["teacher", g, n] = wide.tile([P, PACK * BANK], BF16, name="wide_packed", align_bytes=64)
-            at = BANK * n + 2 * P * half
+        def teacher_rows_sb(g, n):
             if g == 1:
-                rows = teacher_late[:, :, at : at + 2 * P]
-            elif n == 0:
-                rows = teacher_first[:, :, at : at + 2 * P]
-            else:
-                rows = teacher_rest[:, :, at - BANK : at - BANK + 2 * P]
-            interleave(
-                engine,
-                rows,
-                held["teacher", g, n][:, 2 * BANK * half : 2 * BANK * (half + 1)],
+                return teacher_late[:, :, BANK * n : BANK * (n + 1)]
+            if n == 0:
+                return teacher_first[:]
+            return teacher_rest[:, :, BANK * (n - 1) : BANK * n]
+
+        def teacher_tile(g, n):
+            if ("teacher", g, n) not in held:
+                held["teacher", g, n] = wide.tile([P, PACK * BANK], BF16, name="wide_packed", align_bytes=64)
+            return held["teacher", g, n]
+
+        def teacher_pack(engine, g, n, first, last):
+            interleave(engine, teacher_rows_sb(g, n)[:, :, first:last], teacher_tile(g, n)[:, PACK * first : PACK * last])
+
+        def release(slot):
+            nc.vector.memset(ones[:, 8 * slot : 8 * slot + 1], 1.0)
+
+        def teacher_pack_gpsimd(slot, g, n, first, last):
+            nc.gpsimd.tensor_scalar(
+                out=teacher_tile(g, n)[:, PACK * first : PACK * last].rearrange("p (c t) -> p c t", t=PACK),
+                in0=teacher_rows_sb(g, n)[:, :, first:last].rearrange("p t c -> p c t"),
+                scalar1=ones[:, 8 * slot : 8 * slot + 1],
+                scalar2=0.0,
+                op0=MULT,
+                op1=ADD,
             )
 
         def teacher_quantize(g, n):
@@ -259,7 +273,7 @@ def tile_timestep_bias_table_calibration_s8_kernel(
         nc.scalar.activation(out=warm[:, 1:2], in_=warm[:, 0:1], func=SILU)
         nc.sync.dma_start(out=emb_raw[:, 2:4, :], in_=emb_rows[0, :, 2:4, :])
         nc.sync.dma_start(out=w1_raw[:, 1], in_=w1_rows[:, :, BANK:])
-        nc.sync.dma_start(out=teacher_first[:], in_=teacher_rows[0, :, :, :BANK])
+        nc.sync.dma_start(out=teacher_rest[:], in_=teacher_rows[0, :, :, BANK:])
         nc.sync.dma_start(out=emb_raw[:, 4:8, :], in_=emb_rows[1])
         for r in range(4):
             nc.sync.dma_start(
@@ -267,244 +281,253 @@ def tile_timestep_bias_table_calibration_s8_kernel(
                 in_=table_scales[:, r:16:4, :].rearrange("g q c -> q g c").bitcast(I32),
             )
         nc.sync.dma_start(out=table_codes[:], in_=table_words.rearrange("g p n -> p g n"))
-        nc.sync.dma_start(out=teacher_rest[:], in_=teacher_rows[0, :, :, BANK:])
+        nc.sync.dma_start(out=teacher_first[:], in_=teacher_rows[0, :, :, :BANK])
         nc.sync.dma_start(out=teacher_late[:], in_=teacher_rows[1])
         emb_turn(0)
         emb_copy(V, 0)
         w1_pack(V, 0, 0)
-        w1_pack(S, 0, 1)
         emb_turn(1)
+        w1_pack(S, 0, 1)
         emb_quantize(0)
-        w1_quantize(0)
         emb_copy(S, 1)
+        w1_quantize(0)
         hidden(0, 0)
         emb_quantize(1)
-        w1_pack(V, 1, 0)
-        w1_pack(S, 1, 1)
-        silu(0, 0)
         hidden(1, 0)
+        w1_pack(S, 1, 0)
+        silu(0, 0)
+        w1_pack(V, 1, 1)
         silu(1, 0)
-        teacher_pack(V, 0, 0, 0)
         w1_quantize(1)
         hidden(2, 0)
+        teacher_pack(V, 0, 1, 0, 384)
         hidden(3, 0)
-        hidden(0, 1)
-        teacher_pack(V, 0, 0, 1)
         silu(2, 0)
+        hidden(0, 1)
         silu(0, 1)
-        teacher_quantize(0, 0)
         hidden(1, 1)
+        release(0)
+        silu(1, 1)
         factors_turn()
         h_turn(0, 0)
-        silu(1, 1)
+        silu(3, 0)
         h_turn(0, 1)
         hidden(2, 1)
-        a_scale(0, 0)
         hidden(3, 1)
-        silu(3, 0)
         h_turn(1, 0)
+        h_turn(1, 1)
+        teacher_pack(V, 0, 1, 384, 512)
+        silu(2, 1)
+        emb_turn(2)
+        teacher_pack_gpsimd(0, 0, 2, 0, 192)
+        a_scale(0, 0)
         a_scale(0, 1)
         a_quantize(0)
-        a_scale(1, 0)
-        h_turn(1, 1)
-        emb_turn(2)
+        release(1)
         bias_mm(0, 0)
-        silu(3, 1)
-        silu(2, 1)
-        emb_copy(S, 2)
         bias_mm(0, 1)
+        silu(3, 1)
         b_scale(0, 0)
         bias_mm(0, 2)
+        emb_copy(S, 2)
         empty(S, 0, 0, 0)
-        empty(S, 0, 0, 1)
-        empty(S, 0, 0, 2)
+        a_scale(1, 0)
         emb_turn(3)
-        h_turn(2, 0)
         a_scale(1, 1)
+        empty(V, 0, 0, 1)
         emb_quantize(2)
-        a_quantize(1)
-        teacher_pack(S, 0, 1, 0)
+        h_turn(2, 0)
         h_turn(2, 1)
-        emb_copy(S, 3)
-        hidden(4, 0)
-        hidden(4, 1)
-        teacher_pack(V, 0, 2, 0)
-        silu(4, 0)
-        bias_mm(1, 0)
-        bias_mm(1, 1)
+        a_quantize(1)
         a_scale(2, 0)
+        teacher_pack_gpsimd(1, 0, 2, 192, 384)
         b_scale(0, 1)
-        bias_mm(1, 2)
-        silu(4, 1)
-        h_turn(3, 0)
-        h_turn(3, 1)
+        hidden(4, 0)
+        teacher_pack(S, 0, 0, 0, 256)
         a_scale(2, 1)
-        empty(S, 0, 1, 0)
-        emb_quantize(3)
+        hidden(4, 1)
+        bias_mm(1, 0)
+        teacher_pack(V, 1, 0, 0, 192)
+        empty(S, 0, 0, 2)
+        bias_mm(1, 1)
+        emb_copy(S, 3)
+        release(2)
+        silu(4, 1)
+        silu(4, 0)
+        bias_mm(1, 2)
+        h_turn(3, 0)
         a_quantize(2)
-        store(0, 0, 0, 3)
-        empty(S, 0, 1, 1)
+        h_turn(3, 1)
+        empty(S, 0, 1, 0)
         hidden(5, 0)
-        hidden(5, 1)
-        bias_mm(2, 0)
-        bias_mm(2, 1)
-        empty(S, 0, 1, 2)
-        bias_mm(2, 2)
-        h_turn(4, 0)
-        silu(5, 0)
-        teacher_pack(V, 1, 0, 0)
-        empty(S, 0, 2, 0)
         a_scale(3, 0)
         a_scale(3, 1)
-        empty(V, 0, 2, 1)
-        h_turn(4, 1)
+        hidden(5, 1)
+        empty(S, 0, 1, 1)
+        bias_mm(2, 0)
+        emb_quantize(3)
+        empty(S, 0, 1, 2)
+        bias_mm(2, 1)
+        silu(5, 0)
+        bias_mm(2, 2)
+        empty(S, 0, 2, 0)
+        empty(S, 0, 2, 1)
+        h_turn(4, 0)
+        store(0, 0, 0, 3)
+        teacher_quantize(0, 1)
+        release(3)
         a_quantize(3)
+        h_turn(4, 1)
+        a_scale(4, 0)
+        a_scale(4, 1)
+        hidden(6, 0)
         silu(5, 1)
         empty(S, 0, 2, 2)
-        teacher_pack(V, 0, 1, 1)
-        hidden(6, 0)
-        store(0, 1, 0, 3)
         hidden(6, 1)
-        bias_mm(3, 0)
-        a_scale(4, 0)
-        bias_mm(3, 1)
-        a_scale(4, 1)
-        bias_mm(3, 2)
+        teacher_pack(S, 0, 0, 256, 512)
+        teacher_pack(V, 0, 2, 384, 512)
         silu(6, 0)
-        h_turn(5, 0)
-        empty(S, 0, 3, 0)
-        h_turn(5, 1)
-        empty(S, 0, 3, 1)
+        bias_mm(3, 0)
+        bias_mm(3, 1)
         silu(6, 1)
-        teacher_pack(V, 1, 1, 0)
-        hidden(7, 0)
+        bias_mm(3, 2)
+        teacher_pack_gpsimd(2, 1, 0, 192, 384)
+        h_turn(5, 0)
+        h_turn(5, 1)
+        store(0, 1, 0, 3)
+        empty(S, 0, 3, 0)
         a_quantize(4)
-        a_scale(5, 0)
-        empty(S, 0, 3, 2)
-        hidden(7, 1)
-        a_scale(5, 1)
-        teacher_pack(V, 0, 2, 1)
-        teacher_quantize(0, 1)
-        bias_mm(4, 0)
-        bias_mm(4, 1)
-        teacher_pack(V, 1, 0, 1)
-        silu(7, 0)
+        teacher_pack_gpsimd(3, 1, 1, 0, 192)
+        empty(S, 0, 3, 1)
+        hidden(7, 0)
+        release(4)
+        teacher_quantize(0, 2)
+        empty(V, 0, 3, 2)
         store(0, 2, 0, 3)
-        bias_mm(4, 2)
-        a_quantize(5)
+        silu(7, 0)
+        hidden(7, 1)
+        teacher_pack_gpsimd(4, 1, 2, 0, 192)
+        bias_mm(4, 0)
         empty(S, 0, 4, 0)
+        a_scale(5, 0)
+        a_scale(5, 1)
+        bias_mm(4, 1)
+        silu(7, 1)
+        teacher_quantize(0, 0)
+        bias_mm(4, 2)
         h_turn(6, 0)
+        a_quantize(5)
         h_turn(6, 1)
+        bias_mm(5, 0)
+        bias_mm(5, 1)
         empty(S, 0, 4, 1)
         empty(S, 0, 4, 2)
-        bias_mm(5, 0)
-        a_scale(6, 0)
-        a_scale(6, 1)
-        teacher_quantize(0, 2)
-        b_scale(1, 0)
-        teacher_pack(S, 1, 2, 0)
-        a_quantize(6)
-        bias_mm(5, 1)
-        store(0, 3, 0, 3)
-        silu(7, 1)
-        b_quantize(0)
-        teacher_quantize(1, 0)
-        teacher_pack(S, 1, 1, 1)
-        teacher_pack(V, 1, 2, 1)
+        release(5)
         bias_mm(5, 2)
-        teacher_quantize(1, 1)
+        b_scale(1, 0)
+        a_scale(6, 0)
+        empty(S, 0, 5, 0)
+        teacher_pack_gpsimd(5, 1, 1, 192, 384)
+        h_turn(7, 0)
+        h_turn(7, 1)
+        empty(S, 0, 5, 1)
+        empty(S, 0, 5, 2)
+        teacher_pack(S, 1, 0, 384, 512)
+        a_scale(6, 1)
+        teacher_pack(V, 1, 1, 384, 512)
+        release(6)
+        a_quantize(6)
+        a_scale(7, 0)
+        a_scale(7, 1)
+        a_quantize(7)
         bias_mm(6, 0)
         bias_mm(6, 1)
-        empty(S, 0, 5, 0)
-        empty(S, 0, 5, 1)
+        teacher_quantize(1, 0)
         bias_mm(6, 2)
-        teacher_quantize(1, 2)
-        moment_mm(0, 0)
-        moment_mm(0, 1)
-        store(0, 4, 0, 3)
-        b_scale(1, 1)
-        empty(S, 0, 5, 2)
+        bias_mm(7, 0)
         empty(S, 0, 6, 0)
-        moment_mm(0, 2)
+        b_quantize(0)
+        teacher_pack_gpsimd(6, 1, 2, 192, 384)
+        bias_mm(7, 1)
+        teacher_pack(V, 1, 2, 384, 512)
+        teacher_quantize(1, 1)
+        teacher_quantize(1, 2)
+        bias_mm(7, 2)
+        store(0, 3, 0, 3)
+        moment_mm(0, 0)
         empty(S, 0, 6, 1)
+        moment_mm(0, 1)
         empty(S, 0, 6, 2)
-        b_quantize(1)
+        b_scale(1, 1)
+        moment_mm(0, 2)
         moment_mm(1, 0)
-        empty(S, 1, 0, 0)
-        moment_mm(1, 1)
+        empty(S, 0, 7, 0)
+        b_quantize(1)
+        empty(S, 0, 7, 1)
+        store(0, 4, 0, 3)
         b_scale(0, 2)
+        moment_mm(1, 1)
+        empty(S, 0, 7, 2)
         moment_mm(1, 2)
         moment_mm(2, 0)
-        empty(S, 1, 0, 1)
+        empty(S, 1, 0, 0)
         store(0, 5, 0, 3)
-        b_scale(1, 2)
-        store(0, 6, 0, 3)
-        empty(S, 1, 0, 2)
-        empty(S, 1, 1, 0)
+        empty(S, 1, 0, 1)
         moment_mm(2, 1)
+        b_scale(1, 2)
         moment_mm(2, 2)
-        empty(S, 1, 1, 1)
-        empty(V, 1, 2, 0)
-        store(1, 0, 0, 3)
-        empty(S, 1, 1, 2)
-        b_quantize(2)
-        empty(S, 1, 2, 1)
-        b_scale(0, 3)
         moment_mm(3, 0)
+        empty(S, 1, 0, 2)
+        empty(V, 1, 2, 0)
+        empty(S, 1, 1, 0)
+        empty(S, 1, 1, 1)
         moment_mm(3, 1)
+        empty(S, 1, 1, 2)
+        store(0, 6, 0, 3)
+        store(0, 7, 0, 3)
+        b_quantize(2)
         moment_mm(3, 2)
-        moment_mm(4, 0)
-        empty(V, 1, 4, 0)
-        moment_mm(4, 1)
-        moment_mm(4, 2)
+        empty(S, 1, 2, 1)
         empty(S, 1, 2, 2)
+        moment_mm(4, 0)
+        empty(V, 1, 3, 0)
+        b_scale(0, 3)
         b_scale(1, 3)
+        empty(S, 1, 3, 1)
+        b_quantize(3)
+        moment_mm(4, 1)
+        empty(S, 1, 3, 2)
+        moment_mm(4, 2)
+        store(1, 0, 0, 3)
         store(1, 1, 0, 3)
         moment_mm(5, 0)
-        empty(V, 1, 5, 0)
-        empty(S, 1, 3, 0)
-        empty(S, 1, 3, 1)
         moment_mm(5, 1)
-        moment_mm(5, 2)
-        b_quantize(3)
-        h_turn(7, 0)
-        empty(S, 1, 3, 2)
-        h_turn(7, 1)
-        moment_mm(6, 0)
-        a_scale(7, 0)
         store(1, 2, 0, 3)
-        empty(S, 1, 4, 1)
-        empty(S, 1, 4, 2)
-        moment_mm(6, 1)
-        empty(S, 1, 5, 1)
-        moment_mm(6, 2)
-        a_scale(7, 1)
-        empty(S, 1, 5, 2)
+        empty(S, 1, 4, 0)
         store(1, 3, 0, 3)
-        empty(S, 1, 6, 0)
-        store(1, 4, 0, 3)
-        store(1, 5, 0, 3)
+        empty(S, 1, 4, 1)
+        moment_mm(5, 2)
+        moment_mm(6, 0)
+        empty(V, 1, 5, 0)
+        moment_mm(6, 1)
+        moment_mm(6, 2)
+        empty(S, 1, 4, 2)
+        empty(V, 1, 6, 0)
         moment_mm(7, 0)
-        empty(V, 1, 6, 1)
+        empty(S, 1, 5, 1)
+        store(1, 4, 0, 3)
+        empty(S, 1, 5, 2)
+        store(1, 5, 0, 3)
+        empty(S, 1, 6, 1)
         moment_mm(7, 1)
-        empty(V, 1, 6, 2)
-        empty(S, 1, 7, 0)
-        a_quantize(7)
-        empty(V, 1, 7, 1)
-        store(1, 6, 0, 1)
-        store(1, 6, 1, 2)
-        store(1, 6, 2, 3)
         moment_mm(7, 2)
+        empty(V, 1, 7, 0)
+        store(1, 6, 1, 2)
+        store(1, 6, 0, 1)
+        empty(S, 1, 7, 1)
         store(1, 7, 0, 1)
-        bias_mm(7, 0)
-        bias_mm(7, 1)
+        empty(S, 1, 6, 2)
         store(1, 7, 1, 2)
-        empty(V, 1, 7, 2)
+        empty(S, 1, 7, 2)
+        store(1, 6, 2, 3)
         store(1, 7, 2, 3)
-        empty(S, 0, 7, 0)
-        empty(S, 0, 7, 1)
-        bias_mm(7, 2)
-        store(0, 7, 0, 1)
-        store(0, 7, 1, 2)
-        empty(S, 0, 7, 2)
-        store(0, 7, 2, 3)

from contextlib import ExitStack

import concourse.mybir as mybir
from concourse.masks import make_identity

M, K, F, C = 1024, 512, 1024, 1536
FLOPS = 2 * M * K * F + 2 * M * F * C + 2 * F * M * C

F32 = mybir.dt.float32
BF16 = mybir.dt.bfloat16
I32 = mybir.dt.int32
U32 = mybir.dt.uint32
U8 = mybir.dt.uint8
FP8X4 = mybir.dt.float8_e4m3fn_x4
FP4X4 = mybir.dt.float4_e2m1fn_x4
SILU = mybir.ActivationFunctionType.Silu
MULT = mybir.AluOpType.mult
ADD = mybir.AluOpType.add

P = 128
PACK = 4
BANK = 512
CHUNKS = C // BANK


def tile_timestep_bias_table_calibration_s8_kernel(
    tc, emb, w1, gain, table_words, table_scales, level_weight, teacher, out_0, out_1
):
    nc = tc.nc
    emb_rows = emb.rearrange("(g p t) k -> g p t k", g=2, t=PACK)
    w1_rows = w1.rearrange("(p t) f -> p t f", t=PACK)
    teacher_rows = teacher.rearrange("(g p t) c -> g p t c", g=2, t=PACK)
    bias_rows = out_0.rearrange("(g p t) c -> g t p c", g=2, t=PACK)
    moment_rows = out_1.rearrange("(g p t) c -> g t p c", g=2, t=PACK)

    with ExitStack() as ctx:
        keep = ctx.enter_context(tc.tile_pool(name="keep", bufs=1))
        stage = ctx.enter_context(tc.tile_pool(name="stage", bufs=3))
        wide = ctx.enter_context(tc.tile_pool(name="wide", bufs=4))
        results = ctx.enter_context(tc.tile_pool(name="results", bufs=7))
        psum = ctx.enter_context(tc.psum_pool(name="psum", bufs=8))
        ctx.enter_context(tc.manual_schedule())

        ident = keep.tile([P, P], F32, name="ident")
        warm = keep.tile([P, 2], F32, name="warm")
        factor_rows = keep.tile([P, BANK], BF16, name="factor_rows")
        factors = keep.tile([P, 4 * PACK], BF16, name="factors")
        gain_sb = factors[:, : 2 * PACK].rearrange("p (g t) -> p g t", t=PACK)
        level_sb = factors[:, 2 * PACK :].rearrange("p (g t) -> p g t", t=PACK)
        emb_raw = keep.tile([P, 8, K], BF16, name="emb_raw", align_bytes=64)
        w1_raw = keep.tile([P, 2, PACK, BANK], BF16, name="w1_raw", align_bytes=64)
        teacher_first = keep.tile([P, PACK, BANK], BF16, name="teacher_first", align_bytes=64)
        teacher_rest = keep.tile([P, PACK, C - BANK], BF16, name="teacher_rest", align_bytes=64)
        teacher_late = keep.tile([P, PACK, C], BF16, name="teacher_late", align_bytes=64)
        table_codes = keep.tile([P, 2, 2 * C], U8, name="table_codes", align_bytes=64)
        table_plane = keep.tile([P, 2, C], U8, name="table_plane", align_bytes=64)
        emb_codes = keep.tile([P, M], U32, name="emb_codes", align_bytes=64)
        emb_plane = keep.tile([P, M], U8, name="emb_plane", align_bytes=64)
        w1_codes = keep.tile([P, F], U32, name="w1_codes", align_bytes=64)
        w1_plane = keep.tile([P, F], U8, name="w1_plane", align_bytes=64)
        teacher_codes = keep.tile([P, 2, C], U32, name="teacher_codes", align_bytes=64)
        teacher_plane = keep.tile([P, 2, C], U8, name="teacher_plane", align_bytes=64)
        a_codes = keep.tile([P, 8, 2 * P], U32, name="a_codes", align_bytes=64)
        a_plane = keep.tile([P, 8, 2 * P], U8, name="a_plane", align_bytes=64)
        b_codes = keep.tile([P, 4, BANK], U32, name="b_codes", align_bytes=64)
        b_plane = keep.tile([P, 4, BANK], U8, name="b_plane", align_bytes=64)
        h = keep.tile([P, 2, 8, BANK], F32, name="h", align_bytes=64)
        ones = keep.tile([P, 64], F32, name="ones")
        held = {}

        def bank_tile():
            return psum.tile([P, BANK], F32, name="bank")

        def interleave(engine, rows, packed):
            src = rows.rearrange("p t (c i) -> p c t i", i=4)
            dst = packed.rearrange("p (c i t) -> p c t i", i=4, t=PACK)
            if engine is nc.scalar:
                nc.scalar.copy(out=dst, in_=src)
            else:
                nc.vector.tensor_copy(out=dst, in_=src)

        def quantize(codes, plane, packed):
            nc.vector.quantize_mx(out=codes.bitcast(FP8X4), scales=plane, in_=packed)

        def factors_turn():
            bank = bank_tile()
            words = factor_rows[:].bitcast(F32)
            for u in range(2):
                nc.tensor.transpose(bank[:, u * P : (u + 1) * P], words[:, u : 2 * P : 2], ident[:])
            nc.scalar.copy(
                out=factors[:].bitcast(F32).rearrange("p (r u) -> p r u", u=2),
                in_=bank[:, : 2 * P].rearrange("p (u r) -> p r u", u=2)[:, :4, :],
            )

        def emb_turn(pair):
            bank = bank_tile()
            for s in range(2):
                words = emb_raw[:, 2 * pair + s, :].bitcast(F32)
                for u in range(2):
                    at = (2 * s + u) * P
                    nc.tensor.transpose(bank[:, at : at + P], words[:, u : 2 * P : 2], ident[:])
            held["emb_turned", pair] = bank

        def copy(engine, out, in_):
            if engine is nc.scalar:
                nc.scalar.copy(out=out, in_=in_)
            else:
                nc.vector.tensor_copy(out=out, in_=in_)

        def emb_copy(engine, pair):
            bank = held["emb_turned", pair]
            packed = stage.tile([P, 2 * BANK], BF16, name="emb_packed", align_bytes=64)
            copy(
                engine,
                packed[:].bitcast(F32).rearrange("p (s r u) -> p s r u", s=2, u=2),
                bank[:].rearrange("p (s u r) -> p s r u", s=2, u=2),
            )
            held["emb", pair] = packed

        def emb_quantize(pair):
            cols = slice(2 * P * pair, 2 * P * (pair + 1))
            quantize(emb_codes[:, cols], emb_plane[:, cols], held["emb", pair][:])

        def w1_pack(engine, half, part):
            if part == 0:
                held["w1", half] = wide.tile([P, PACK * BANK], BF16, name="wide_packed", align_bytes=64)
            copy(
                engine,
                held["w1", half][:, 2 * BANK * part : 2 * BANK * (part + 1)].rearrange("p (t m j) -> p t m j", t=2, j=PACK),
                w1_raw[:, half].rearrange("p j (m t) -> p t m j", t=PACK)[:, 2 * part : 2 * part + 2],
            )

        def w1_quantize(half):
            cols = slice(BANK * half, BANK * (half + 1))
            quantize(w1_codes[:, cols], w1_plane[:, cols], held["w1", half][:])

        def teacher_rows_sb(g, n):
            if g == 1:
                return teacher_late[:, :, BANK * n : BANK * (n + 1)]
            if n == 0:
                return teacher_first[:]
            return teacher_rest[:, :, BANK * (n - 1) : BANK * n]

        def teacher_tile(g, n):
            if ("teacher", g, n) not in held:
                held["teacher", g, n] = wide.tile([P, PACK * BANK], BF16, name="wide_packed", align_bytes=64)
            return held["teacher", g, n]

        def teacher_pack(engine, g, n, first, last):
            interleave(engine, teacher_rows_sb(g, n)[:, :, first:last], teacher_tile(g, n)[:, PACK * first : PACK * last])

        def release(slot):
            nc.vector.memset(ones[:, 8 * slot : 8 * slot + 1], 1.0)

        def teacher_pack_gpsimd(slot, g, n, first, last):
            nc.gpsimd.tensor_scalar(
                out=teacher_tile(g, n)[:, PACK * first : PACK * last].rearrange("p (c t) -> p c t", t=PACK),
                in0=teacher_rows_sb(g, n)[:, :, first:last].rearrange("p t c -> p c t"),
                scalar1=ones[:, 8 * slot : 8 * slot + 1],
                scalar2=0.0,
                op0=MULT,
                op1=ADD,
            )

        def teacher_quantize(g, n):
            cols = slice(BANK * n, BANK * (n + 1))
            quantize(teacher_codes[:, g, cols], teacher_plane[:, g, cols], held["teacher", g, n][:])

        def hidden(i, half):
            rows = slice(P * i, P * (i + 1))
            cols = slice(BANK * half, BANK * (half + 1))
            bank = bank_tile()
            nc.tensor.matmul_mx(
                out=bank[:],
                lhsT=emb_codes[:, rows].bitcast(FP8X4),
                lhsT_scale=emb_plane[:, rows],
                rhs=w1_codes[:, cols].bitcast(FP8X4),
                rhs_scale=w1_plane[:, cols],
                start=True,
                stop=True,
            )
            held["z", i, half] = bank

        def silu(i, half):
            bank = held["z", i, half]
            nc.scalar.activation(
                out=h[:, half, i, :],
                in_=bank[:],
                func=SILU,
            )

        def h_turn(i, half):
            bank = bank_tile()
            for t in range(PACK):
                nc.tensor.transpose(bank[:, P * t : P * (t + 1)], h[:, half, i, P * t : P * (t + 1)], ident[:])
            held["turned", i, half] = bank

        def a_scale(i, half):
            if half == 0:
                held["a", i] = stage.tile([P, 2 * BANK], BF16, name="a_packed", align_bytes=64)
            nc.vector.tensor_tensor(
                out=held["a", i][:, BANK * half : BANK * (half + 1)].rearrange("p (n t) -> p n t", t=PACK),
                in0=held["turned", i, half][:].rearrange("p (t n) -> p n t", t=PACK),
                in1=gain_sb[:, half, :].unsqueeze(1).to_broadcast([P, P, PACK]),
                op=MULT,
            )

        def a_quantize(i):
            quantize(a_codes[:, i, :], a_plane[:, i, :], held["a", i][:])

        def b_scale(g, q):
            if g == 0:
                held["b", q] = wide.tile([P, PACK * BANK], BF16, name="b_packed", align_bytes=64)
            rows = h[:, q // 2, PACK * g : PACK * (g + 1), 2 * P * (q % 2) : 2 * P * (q % 2 + 1)]
            nc.vector.tensor_tensor(
                out=held["b", q][:, 2 * BANK * g : 2 * BANK * (g + 1)].rearrange("p (c i t) -> p c t i", i=2, t=PACK),
                in0=rows.rearrange("p t (c i) -> p c t i", i=2),
                in1=level_sb[:, g, :].unsqueeze(1).unsqueeze(3).to_broadcast([P, P, PACK, 2]),
                op=MULT,
            )

        def b_quantize(q):
            quantize(b_codes[:, q, :], b_plane[:, q, :], held["b", q][:])

        def bias_mm(i, n):
            bank = bank_tile()
            for g in range(2):
                nc.tensor.matmul_mx(
                    out=bank[:],
                    lhsT=a_codes[:, i, P * g : P * (g + 1)].bitcast(FP8X4),
                    lhsT_scale=a_plane[:, i, P * g : P * (g + 1)],
                    rhs=table_codes[:, g, 2 * BANK * n : 2 * BANK * (n + 1)].bitcast(FP4X4),
                    rhs_scale=table_plane[:, g, BANK * n : BANK * (n + 1)],
                    start=(g == 0),
                    stop=(g == 1),
                )
            held["sum", 0, i, n] = bank

        def moment_mm(j, n):
            bank = bank_tile()
            for g in range(2):
                at = 2 * P * g + P * (j % 2)
                nc.tensor.matmul_mx(
                    out=bank[:],
                    lhsT=b_codes[:, j // 2, at : at + P].bitcast(FP8X4),
                    lhsT_scale=b_plane[:, j // 2, at : at + P],
                    rhs=teacher_codes[:, g, BANK * n : BANK * (n + 1)].bitcast(FP8X4),
                    rhs_scale=teacher_plane[:, g, BANK * n : BANK * (n + 1)],
                    start=(g == 0),
                    stop=(g == 1),
                )
            held["sum", 1, j, n] = bank

        def empty(engine, which, i, n):
            if n == 0:
                held["result", which, i] = results.tile([P, C], F32, name="result")
            copy(engine, held["result", which, i][:, BANK * n : BANK * (n + 1)], held["sum", which, i, n][:])

        def store(which, i, first, last):
            rows = (bias_rows, moment_rows)[which][i // PACK, i % PACK]
            cols = slice(BANK * first, BANK * last)
            nc.sync.dma_start(out=rows[:, cols], in_=held["result", which, i][:, cols])

        V, S = nc.vector, nc.scalar
        nc.sync.dma_start(out=emb_raw[:, 0:2, :], in_=emb_rows[0, :, 0:2, :])
        nc.sync.dma_start(out=w1_raw[:, 0], in_=w1_rows[:, :, :BANK])
        nc.vector.memset(factor_rows[:].bitcast(I32), 0)
        nc.scalar.dma_start(out=factor_rows[0:2, :], in_=gain.rearrange("(g k) -> g k", g=2))
        nc.scalar.dma_start(out=factor_rows[2:4, :], in_=level_weight.rearrange("(g k) -> g k", g=2))
        nc.vector.memset(table_plane[:].rearrange("p g c -> p (g c)").bitcast(I32), 0)
        nc.vector.memset(warm[:], 0.0)
        make_identity(nc, ident[:])
        nc.scalar.activation(out=warm[:, 1:2], in_=warm[:, 0:1], func=SILU)
        nc.sync.dma_start(out=emb_raw[:, 2:4, :], in_=emb_rows[0, :, 2:4, :])
        nc.sync.dma_start(out=w1_raw[:, 1], in_=w1_rows[:, :, BANK:])
        nc.sync.dma_start(out=teacher_rest[:], in_=teacher_rows[0, :, :, BANK:])
        nc.sync.dma_start(out=emb_raw[:, 4:8, :], in_=emb_rows[1])
        for r in range(4):
            nc.sync.dma_start(
                out=table_plane[r:P:32].bitcast(I32),
                in_=table_scales[:, r:16:4, :].rearrange("g q c -> q g c").bitcast(I32),
            )
        nc.sync.dma_start(out=table_codes[:], in_=table_words.rearrange("g p n -> p g n"))
        nc.sync.dma_start(out=teacher_first[:], in_=teacher_rows[0, :, :, :BANK])
        nc.sync.dma_start(out=teacher_late[:], in_=teacher_rows[1])
        emb_turn(0)
        emb_copy(V, 0)
        w1_pack(V, 0, 0)
        emb_turn(1)
        w1_pack(S, 0, 1)
        emb_quantize(0)
        emb_copy(S, 1)
        w1_quantize(0)
        hidden(0, 0)
        emb_quantize(1)
        hidden(1, 0)
        w1_pack(S, 1, 0)
        silu(0, 0)
        w1_pack(V, 1, 1)
        silu(1, 0)
        w1_quantize(1)
        hidden(2, 0)
        teacher_pack(V, 0, 1, 0, 384)
        hidden(3, 0)
        silu(2, 0)
        hidden(0, 1)
        silu(0, 1)
        hidden(1, 1)
        release(0)
        silu(1, 1)
        factors_turn()
        h_turn(0, 0)
        silu(3, 0)
        h_turn(0, 1)
        hidden(2, 1)
        hidden(3, 1)
        h_turn(1, 0)
        h_turn(1, 1)
        teacher_pack(V, 0, 1, 384, 512)
        silu(2, 1)
        emb_turn(2)
        teacher_pack_gpsimd(0, 0, 2, 0, 192)
        a_scale(0, 0)
        a_scale(0, 1)
        a_quantize(0)
        release(1)
        bias_mm(0, 0)
        bias_mm(0, 1)
        silu(3, 1)
        b_scale(0, 0)
        bias_mm(0, 2)
        emb_copy(S, 2)
        empty(S, 0, 0, 0)
        a_scale(1, 0)
        emb_turn(3)
        a_scale(1, 1)
        empty(V, 0, 0, 1)
        emb_quantize(2)
        h_turn(2, 0)
        h_turn(2, 1)
        a_quantize(1)
        a_scale(2, 0)
        teacher_pack_gpsimd(1, 0, 2, 192, 384)
        b_scale(0, 1)
        hidden(4, 0)
        teacher_pack(S, 0, 0, 0, 256)
        a_scale(2, 1)
        hidden(4, 1)
        bias_mm(1, 0)
        teacher_pack(V, 1, 0, 0, 192)
        empty(S, 0, 0, 2)
        bias_mm(1, 1)
        emb_copy(S, 3)
        release(2)
        silu(4, 1)
        silu(4, 0)
        bias_mm(1, 2)
        h_turn(3, 0)
        a_quantize(2)
        h_turn(3, 1)
        empty(S, 0, 1, 0)
        hidden(5, 0)
        a_scale(3, 0)
        a_scale(3, 1)
        hidden(5, 1)
        empty(S, 0, 1, 1)
        bias_mm(2, 0)
        emb_quantize(3)
        empty(S, 0, 1, 2)
        bias_mm(2, 1)
        silu(5, 0)
        bias_mm(2, 2)
        empty(S, 0, 2, 0)
        empty(S, 0, 2, 1)
        h_turn(4, 0)
        store(0, 0, 0, 3)
        teacher_quantize(0, 1)
        release(3)
        a_quantize(3)
        h_turn(4, 1)
        a_scale(4, 0)
        a_scale(4, 1)
        hidden(6, 0)
        silu(5, 1)
        empty(S, 0, 2, 2)
        hidden(6, 1)
        teacher_pack(S, 0, 0, 256, 512)
        teacher_pack(V, 0, 2, 384, 512)
        silu(6, 0)
        bias_mm(3, 0)
        bias_mm(3, 1)
        silu(6, 1)
        bias_mm(3, 2)
        teacher_pack_gpsimd(2, 1, 0, 192, 384)
        h_turn(5, 0)
        h_turn(5, 1)
        store(0, 1, 0, 3)
        empty(S, 0, 3, 0)
        a_quantize(4)
        teacher_pack_gpsimd(3, 1, 1, 0, 192)
        empty(S, 0, 3, 1)
        hidden(7, 0)
        release(4)
        teacher_quantize(0, 2)
        empty(V, 0, 3, 2)
        store(0, 2, 0, 3)
        silu(7, 0)
        hidden(7, 1)
        teacher_pack_gpsimd(4, 1, 2, 0, 192)
        bias_mm(4, 0)
        empty(S, 0, 4, 0)
        a_scale(5, 0)
        a_scale(5, 1)
        bias_mm(4, 1)
        silu(7, 1)
        teacher_quantize(0, 0)
        bias_mm(4, 2)
        h_turn(6, 0)
        a_quantize(5)
        h_turn(6, 1)
        bias_mm(5, 0)
        bias_mm(5, 1)
        empty(S, 0, 4, 1)
        empty(S, 0, 4, 2)
        release(5)
        bias_mm(5, 2)
        b_scale(1, 0)
        a_scale(6, 0)
        empty(S, 0, 5, 0)
        teacher_pack_gpsimd(5, 1, 1, 192, 384)
        h_turn(7, 0)
        h_turn(7, 1)
        empty(S, 0, 5, 1)
        empty(S, 0, 5, 2)
        teacher_pack(S, 1, 0, 384, 512)
        a_scale(6, 1)
        teacher_pack(V, 1, 1, 384, 512)
        release(6)
        a_quantize(6)
        a_scale(7, 0)
        a_scale(7, 1)
        a_quantize(7)
        bias_mm(6, 0)
        bias_mm(6, 1)
        teacher_quantize(1, 0)
        bias_mm(6, 2)
        bias_mm(7, 0)
        empty(S, 0, 6, 0)
        b_quantize(0)
        teacher_pack_gpsimd(6, 1, 2, 192, 384)
        bias_mm(7, 1)
        teacher_pack(V, 1, 2, 384, 512)
        teacher_quantize(1, 1)
        teacher_quantize(1, 2)
        bias_mm(7, 2)
        store(0, 3, 0, 3)
        moment_mm(0, 0)
        empty(S, 0, 6, 1)
        moment_mm(0, 1)
        empty(S, 0, 6, 2)
        b_scale(1, 1)
        moment_mm(0, 2)
        moment_mm(1, 0)
        empty(S, 0, 7, 0)
        b_quantize(1)
        empty(S, 0, 7, 1)
        store(0, 4, 0, 3)
        b_scale(0, 2)
        moment_mm(1, 1)
        empty(S, 0, 7, 2)
        moment_mm(1, 2)
        moment_mm(2, 0)
        empty(S, 1, 0, 0)
        store(0, 5, 0, 3)
        empty(S, 1, 0, 1)
        moment_mm(2, 1)
        b_scale(1, 2)
        moment_mm(2, 2)
        moment_mm(3, 0)
        empty(S, 1, 0, 2)
        empty(V, 1, 2, 0)
        empty(S, 1, 1, 0)
        empty(S, 1, 1, 1)
        moment_mm(3, 1)
        empty(S, 1, 1, 2)
        store(0, 6, 0, 3)
        store(0, 7, 0, 3)
        b_quantize(2)
        moment_mm(3, 2)
        empty(S, 1, 2, 1)
        empty(S, 1, 2, 2)
        moment_mm(4, 0)
        empty(V, 1, 3, 0)
        b_scale(0, 3)
        b_scale(1, 3)
        empty(S, 1, 3, 1)
        b_quantize(3)
        moment_mm(4, 1)
        empty(S, 1, 3, 2)
        moment_mm(4, 2)
        store(1, 0, 0, 3)
        store(1, 1, 0, 3)
        moment_mm(5, 0)
        moment_mm(5, 1)
        store(1, 2, 0, 3)
        empty(S, 1, 4, 0)
        store(1, 3, 0, 3)
        empty(S, 1, 4, 1)
        moment_mm(5, 2)
        moment_mm(6, 0)
        empty(V, 1, 5, 0)
        moment_mm(6, 1)
        moment_mm(6, 2)
        empty(S, 1, 4, 2)
        empty(V, 1, 6, 0)
        moment_mm(7, 0)
        empty(S, 1, 5, 1)
        store(1, 4, 0, 3)
        empty(S, 1, 5, 2)
        store(1, 5, 0, 3)
        empty(S, 1, 6, 1)
        moment_mm(7, 1)
        moment_mm(7, 2)
        empty(V, 1, 7, 0)
        store(1, 6, 1, 2)
        store(1, 6, 0, 1)
        empty(S, 1, 7, 1)
        store(1, 7, 0, 1)
        empty(S, 1, 6, 2)
        store(1, 7, 1, 2)
        empty(S, 1, 7, 2)
        store(1, 6, 2, 3)
        store(1, 7, 2, 3)
